import numpy as np
CORES = [51,54,179,182]
N = 4
TK = 256
D = 128 * N
EPS = 0.01
def setup_inputs(rng):
    return {"x": (rng.standard_normal((N, 128, TK), dtype=np.float32) * (0.5 + np.abs(rng.standard_normal((1, 1, TK), dtype=np.float32))) + rng.standard_normal((1, 1, TK), dtype=np.float32))}
def reference(x):
    X = x.astype(np.float64)
    mu = X.sum(axis=(0, 1)) / D
    Z = X - mu
    Z = Z / np.sqrt((Z ** 2).sum(axis=(0, 1)) / D + EPS)
    return {"y": Z.astype(np.float32)}

@@ -1,0 +1,163 @@
+import numpy as np
+from concourse.bass import DstId, RemoteDMATransfer
+from concourse.mybir import AluOpType, AxisListType, ActivationFunctionType
+
+EPS = 0.01
+K = 24
+DEG = 13
+L = DEG + 2
+TAU = 0.036
+CEN = 5.0 / 3.0
+SIG = float(np.sqrt(8.0 / (3.0 * TAU)))
+
+
+def _coefs():
+    ch = np.polynomial.chebyshev.Chebyshev.interpolate(lambda z: (CEN - z) ** -0.5, DEG, domain=[-1.08, 1.08])
+    return [float(c) for c in ch.convert(kind=np.polynomial.Polynomial, domain=[-1, 1], window=[-1, 1]).coef]
+
+
+SCRATCH = {
+    "xs": ("sbuf", [128, 256], "float32"),
+    "sq": ("sbuf", [128, 256], "float32"),
+    "cvec": ("sbuf", [128, 2], "float32"),
+    "epsadd": ("sbuf", [128, 4], "float32"),
+    "buf": ("sbuf", [128, 16], "float32"),
+    "ones": ("sbuf", [128, 128], "float32"),
+    "ident": ("sbuf", [128, 128], "float32"),
+    "t8": ("sbuf", [128, 8], "float32"),
+    "tot": ("sbuf", [128, 4], "float32"),
+    "nv": ("sbuf", [128, 2], "float32"),
+    "four": ("sbuf", [128, K], "float32"),
+    "zero": ("sbuf", [128, K], "float32"),
+    "tneg": ("sbuf", [128, K], "float32"),
+    "fb": ("sbuf", [128, 2 * (K + 1)], "float32"),
+    "gg": ("sbuf", [128, 2], "float32"),
+    "d0": ("sbuf", [128, 2 * L], "float32"),
+    "d1": ("sbuf", [128, 2 * L], "float32"),
+    "rs": ("sbuf", [128, 2 * L], "float32"),
+    "yt": ("sbuf", [128, 256], "float32"),
+    "ys": ("sbuf", [128, 256], "float32"),
+    "ps_stat": ("psum", [128, 512], "float32"),
+    "ps_xt": ("psum", [128, 512], "float32"),
+    "ps_y0": ("psum", [128, 512], "float32"),
+    "ps_y1": ("psum", [128, 512], "float32"),
+}
+SEMAPHORES = ["ld", "crhs", "cones", "idn", "sqd", "mm", "slot", "dv", "arr", "sent", "xt",
+              "ap0", "ap1", "ty0", "ty1", "cp0", "cp1", "st"]
+
+
+def rank_program(g, core, T, topo):
+    rank = T.rank_of(core)
+    if rank is None:
+        return
+    S = T.sem
+    v, pe, act, sy = g.vector, g.tensor, g.scalar, g.sync
+    n = len(T.cores)
+    d = 128 * n
+    others = [c for c in T.cores if c != core]
+    A = AluOpType
+    co = _coefs()
+    cnt = [0]
+
+    def dv(ins):
+        ins.then_inc(S.dv, 1)
+        cnt[0] += 1
+
+    def vsync():
+        v.wait_ge(S.dv, cnt[0])
+
+    sy.dma_start(T.xs[:], T.x[:]).then_inc(S.ld, 16)
+
+    v.memset(T.cvec[:, 0:1], 1.0 / d).then_inc(S.crhs, 1)
+    v.memset(T.cvec[:, 1:2], -1.0 / d).then_inc(S.crhs, 1)
+    v.memset(T.ones[:], 1.0).then_inc(S.cones, 1)
+    dv(v.memset(T.epsadd[:, 0:2], 0.0))
+    dv(v.memset(T.epsadd[:, 2:4], -EPS / n))
+    g.wait_ge(S.cones, 1)
+    g.affine_select(T.ident[:], T.ones[:], [[-1, 128]], A.is_equal, 0.0, 0, 1).then_inc(S.idn, 1)
+
+    act.wait_ge(S.ld, 16)
+    act.activation(T.sq[:], T.xs[:], ActivationFunctionType.Square).then_inc(S.sqd, 1)
+    pe.wait_ge(S.ld, 16)
+    pe.wait_ge(S.crhs, 2)
+    for h in range(2):
+        pe.matmul(T.ps_stat[:, h:h + 1], T.xs[:, 128 * h:128 * h + 128], T.cvec[:, 0:1], True, True).then_inc(S.mm, 1)
+    pe.wait_ge(S.sqd, 1)
+    for h in range(2):
+        pe.matmul(T.ps_stat[:, 2 + h:3 + h], T.sq[:, 128 * h:128 * h + 128], T.cvec[:, 1:2], True, True).then_inc(S.mm, 1)
+    v.wait_ge(S.mm, 4)
+    vsync()
+    mine = T.buf[:, 4 * rank:4 * rank + 4]
+    v.tensor_tensor(mine, T.ps_stat[:, 0:4], T.epsadd[:], A.add).then_inc(S.slot, 1)
+
+    mask = -1
+    for c in others:
+        mask &= topo.mask(core, c)
+    ne = bin(mask).count("1")
+    ids = []
+    for c in others:
+        rid, pid = topo.addr(c, core)
+        ids.append(DstId(rid=rid, pnc=pid))
+    g.wait_ge(S.slot, 1)
+    g.remote_dma_fused([RemoteDMATransfer(dst_ids=ids, dma_engine_mask=mask, remote_sem=S.arr, srcs=[mine],
+                                          dsts=[mine for _ in others], alu_op=0)], local_sem=S.sent)
+
+    pe.wait_ge(S.idn, 1)
+    for h in range(2):
+        pe.transpose(T.ps_xt[:, 128 * h:128 * h + 128], T.xs[:, 128 * h:128 * h + 128], T.ident[:]).then_inc(S.xt, 1)
+    dv(v.memset(T.four[:], 4.0))
+    dv(v.memset(T.zero[:], 0.0))
+    vsync()
+    dv(v.tensor_tensor_scan(T.tneg[:], T.four[:], T.zero[:], -TAU / 4.0, A.mult, A.add))
+    dv(v.memset(T.fb[:, K::K + 1], SIG))
+    dv(v.memset(T.d0[:, 0::L], 0.0))
+    dv(v.memset(T.d1[:, DEG + 1::L], 0.0))
+    for j in range(DEG + 1):
+        dv(v.memset(T.d1[:, j::L], co[DEG - j]))
+
+    v.wait_ge(S.arr, ne * len(others))
+    v.wait_ge(S.slot, 1)
+    v.wait_ge(S.cones, 1)
+    dv(v.tensor_tensor(T.t8[:], T.buf[:, 0:8], T.buf[:, 8:16], A.add))
+    vsync()
+    dv(v.tensor_tensor(T.tot[:], T.t8[:, 0:4], T.t8[:, 4:8], A.add))
+    vsync()
+    for h in range(2):
+        dv(v.tensor_scalar(T.nv[:, h:h + 1], T.tot[:, h:h + 1], T.tot[:, h:h + 1], T.tot[:, 2 + h:3 + h], A.mult, A.add))
+    vsync()
+    for h in range(2):
+        o = h * (K + 1)
+        dv(v.tensor_scalar(T.fb[:, o:o + K], T.tneg[:], T.nv[:, h:h + 1], 0.5, A.is_lt, A.max))
+    vsync()
+    for h in range(2):
+        o = h * (K + 1)
+        dv(v.tensor_reduce(T.d0[:, h * L + DEG + 1:h * L + DEG + 2], T.fb[:, o:o + K + 1], AxisListType.X, A.mult))
+    vsync()
+    for h in range(2):
+        y0 = T.d0[:, h * L + DEG + 1:h * L + DEG + 2]
+        dv(v.tensor_scalar(T.gg[:, h:h + 1], T.nv[:, h:h + 1], y0, y0, A.mult, A.mult))
+    vsync()
+    for h in range(2):
+        dv(v.tensor_scalar(T.d0[:, h * L + 1:h * L + 1 + DEG], T.ones[:, 0:DEG], T.gg[:, h:h + 1], CEN, A.mult, A.add))
+    vsync()
+    dv(v.tensor_tensor_scan(T.rs[:], T.d0[:], T.d1[:], 0.0, A.mult, A.add))
+    vsync()
+    v.wait_ge(S.xt, 2)
+    for h, ap in ((0, S.ap0), (1, S.ap1)):
+        v.tensor_scalar(T.yt[:, 128 * h:128 * h + 128], T.ps_xt[:, 128 * h:128 * h + 128], T.tot[:, h:h + 1],
+                        T.rs[:, h * L + L - 1:h * L + L], A.subtract, A.mult).then_inc(ap, 1)
+
+    pe.wait_ge(S.ap0, 1)
+    pe.transpose(T.ps_y0[:, 0:128], T.yt[:, 0:128], T.ident[:]).then_inc(S.ty0, 1)
+    pe.wait_ge(S.ap1, 1)
+    pe.transpose(T.ps_y1[:, 0:128], T.yt[:, 128:256], T.ident[:]).then_inc(S.ty1, 1)
+    v.wait_ge(S.ty0, 1)
+    v.tensor_copy(T.ys[:, 0:128], T.ps_y0[:, 0:128]).then_inc(S.cp0, 1)
+    v.wait_ge(S.ty1, 1)
+    v.tensor_copy(T.ys[:, 128:256], T.ps_y1[:, 0:128]).then_inc(S.cp1, 1)
+    sy.wait_ge(S.cp0, 1)
+    sy.dma_start(T.y[:, 0:128], T.ys[:, 0:128]).then_inc(S.st, 16)
+    act.wait_ge(S.cp1, 1)
+    act.dma_start(T.y[:, 128:256], T.ys[:, 128:256]).then_inc(S.st, 16)
+    g.wait_ge(S.sent, ne)
+    sy.wait_ge(S.st, 32)

@@ -3,16 +3,19 @@ from concourse.bass import DstId, RemoteDMATransfer
 from concourse.mybir import AluOpType, AxisListType, ActivationFunctionType
 
 EPS = 0.01
-K = 24
-DEG = 13
-L = DEG + 2
+K = 31
+DEG = 11
 TAU = 0.036
-CEN = 5.0 / 3.0
-SIG = float(np.sqrt(8.0 / (3.0 * TAU)))
+S2 = 64.0
+CEN = S2 * TAU * 5.0 / 8.0
+HW = S2 * TAU * 3.0 / 8.0
+LA = K + 2 + DEG
+LB = DEG + 1 + K
 
 
 def _coefs():
-    ch = np.polynomial.chebyshev.Chebyshev.interpolate(lambda z: (CEN - z) ** -0.5, DEG, domain=[-1.08, 1.08])
+    ch = np.polynomial.chebyshev.Chebyshev.interpolate(lambda z: (CEN - z) ** -0.5 * np.sqrt(S2), DEG,
+                                                       domain=[-1.04 * HW, 1.04 * HW])
     return [float(c) for c in ch.convert(kind=np.polynomial.Polynomial, domain=[-1, 1], window=[-1, 1]).coef]
 
 
@@ -24,17 +27,17 @@ SCRATCH = {
     "buf": ("sbuf", [128, 16], "float32"),
     "ones": ("sbuf", [128, 128], "float32"),
     "ident": ("sbuf", [128, 128], "float32"),
-    "t8": ("sbuf", [128, 8], "float32"),
     "tot": ("sbuf", [128, 4], "float32"),
-    "nv": ("sbuf", [128, 2], "float32"),
     "four": ("sbuf", [128, K], "float32"),
-    "zero": ("sbuf", [128, K], "float32"),
     "tneg": ("sbuf", [128, K], "float32"),
-    "fb": ("sbuf", [128, 2 * (K + 1)], "float32"),
-    "gg": ("sbuf", [128, 2], "float32"),
-    "d0": ("sbuf", [128, 2 * L], "float32"),
-    "d1": ("sbuf", [128, 2 * L], "float32"),
-    "rs": ("sbuf", [128, 2 * L], "float32"),
+    "a0": ("sbuf", [128, LA], "float32"),
+    "a1": ("sbuf", [128, LA], "float32"),
+    "da": ("sbuf", [128, LA], "float32"),
+    "b0": ("sbuf", [128, LA + K], "float32"),
+    "b1": ("sbuf", [128, LA + K], "float32"),
+    "db": ("sbuf", [128, LB], "float32"),
+    "r0": ("sbuf", [128, LB], "float32"),
+    "r1": ("sbuf", [128, LB], "float32"),
     "yt": ("sbuf", [128, 256], "float32"),
     "ys": ("sbuf", [128, 256], "float32"),
     "ps_stat": ("psum", [128, 512], "float32"),
@@ -42,7 +45,7 @@ SCRATCH = {
     "ps_y0": ("psum", [128, 512], "float32"),
     "ps_y1": ("psum", [128, 512], "float32"),
 }
-SEMAPHORES = ["ld", "crhs", "cones", "idn", "sqd", "mm", "slot", "dv", "arr", "sent", "xt",
+SEMAPHORES = ["ld", "crhs", "cones", "idn", "sq0", "sq1", "mm", "slot", "dvc", "h0", "h1", "arr", "sent", "xt",
               "ap0", "ap1", "ty0", "ty1", "cp0", "cp1", "st"]
 
 
@@ -54,39 +57,54 @@ def rank_program(g, core, T, topo):
     v, pe, act, sy = g.vector, g.tensor, g.scalar, g.sync
     n = len(T.cores)
     d = 128 * n
-    others = [c for c in T.cores if c != core]
     A = AluOpType
     co = _coefs()
-    cnt = [0]
 
-    def dv(ins):
-        ins.then_inc(S.dv, 1)
-        cnt[0] += 1
+    def place(c):
+        return (topo.host(c), topo.chip(c))
 
-    def vsync():
-        v.wait_ge(S.dv, cnt[0])
+    others = [c for c in T.cores if c != core and place(c) != place(core)]
+    others += [c for c in T.cores if c != core and place(c) == place(core)]
 
     sy.dma_start(T.xs[:], T.x[:]).then_inc(S.ld, 16)
+
+    cc = [0]
+
+    def cst(ins):
+        ins.then_inc(S.dvc, 1)
+        cc[0] += 1
 
     v.memset(T.cvec[:, 0:1], 1.0 / d).then_inc(S.crhs, 1)
     v.memset(T.cvec[:, 1:2], -1.0 / d).then_inc(S.crhs, 1)
     v.memset(T.ones[:], 1.0).then_inc(S.cones, 1)
-    dv(v.memset(T.epsadd[:, 0:2], 0.0))
-    dv(v.memset(T.epsadd[:, 2:4], -EPS / n))
     g.wait_ge(S.cones, 1)
     g.affine_select(T.ident[:], T.ones[:], [[-1, 128]], A.is_equal, 0.0, 0, 1).then_inc(S.idn, 1)
+    cst(v.memset(T.four[:], 4.0))
+    cst(v.memset(T.da[:, 0:K + 1], 0.0))
+    cst(v.memset(T.epsadd[:, 0:2], 0.0))
+    cst(v.memset(T.epsadd[:, 2:4], -EPS / n))
+    cst(v.memset(T.da[:, K + 1:K + 2], CEN))
+    cst(v.memset(T.da[:, K + 2:LA], 0.0))
+    cst(v.memset(T.a0[:, K + 1:LA], 1.0))
+    cst(v.memset(T.a1[:, K + 1:LA], 1.0))
+    cst(v.memset(T.db[:, DEG + 1:LB], 0.0))
+    for j in range(DEG + 1):
+        cst(v.memset(T.db[:, j:j + 1], co[DEG - j]))
+    v.wait_ge(S.dvc, cc[0])
+    cst(v.tensor_tensor_scan(T.tneg[:], T.four[:], T.da[:, 0:K], -TAU / 4.0, A.mult, A.add))
 
     act.wait_ge(S.ld, 16)
-    act.activation(T.sq[:], T.xs[:], ActivationFunctionType.Square).then_inc(S.sqd, 1)
+    for h, s in ((0, S.sq0), (1, S.sq1)):
+        act.activation(T.sq[:, 128 * h:128 * h + 128], T.xs[:, 128 * h:128 * h + 128],
+                       ActivationFunctionType.Square).then_inc(s, 1)
     pe.wait_ge(S.ld, 16)
     pe.wait_ge(S.crhs, 2)
     for h in range(2):
         pe.matmul(T.ps_stat[:, h:h + 1], T.xs[:, 128 * h:128 * h + 128], T.cvec[:, 0:1], True, True).then_inc(S.mm, 1)
-    pe.wait_ge(S.sqd, 1)
-    for h in range(2):
+    for h, s in ((0, S.sq0), (1, S.sq1)):
+        pe.wait_ge(s, 1)
         pe.matmul(T.ps_stat[:, 2 + h:3 + h], T.sq[:, 128 * h:128 * h + 128], T.cvec[:, 1:2], True, True).then_inc(S.mm, 1)
     v.wait_ge(S.mm, 4)
-    vsync()
     mine = T.buf[:, 4 * rank:4 * rank + 4]
     v.tensor_tensor(mine, T.ps_stat[:, 0:4], T.epsadd[:], A.add).then_inc(S.slot, 1)
 
@@ -105,47 +123,38 @@ def rank_program(g, core, T, topo):
     pe.wait_ge(S.idn, 1)
     for h in range(2):
         pe.transpose(T.ps_xt[:, 128 * h:128 * h + 128], T.xs[:, 128 * h:128 * h + 128], T.ident[:]).then_inc(S.xt, 1)
-    dv(v.memset(T.four[:], 4.0))
-    dv(v.memset(T.zero[:], 0.0))
-    vsync()
-    dv(v.tensor_tensor_scan(T.tneg[:], T.four[:], T.zero[:], -TAU / 4.0, A.mult, A.add))
-    dv(v.memset(T.fb[:, K::K + 1], SIG))
-    dv(v.memset(T.d0[:, 0::L], 0.0))
-    dv(v.memset(T.d1[:, DEG + 1::L], 0.0))
-    for j in range(DEG + 1):
-        dv(v.memset(T.d1[:, j::L], co[DEG - j]))
 
-    v.wait_ge(S.arr, ne * len(others))
+    half = ((0, T.a0, T.b0, T.r0, S.h0, S.ap0), (1, T.a1, T.b1, T.r1, S.h1, S.ap1))
+    hc = [0, 0]
+
+    def step(h, sem, calls):
+        if hc[h]:
+            v.wait_ge(sem, hc[h])
+        for ins in calls():
+            ins.then_inc(sem, 1)
+            hc[h] += 1
+
+    v.wait_ge(S.dvc, cc[0])
     v.wait_ge(S.slot, 1)
-    v.wait_ge(S.cones, 1)
-    dv(v.tensor_tensor(T.t8[:], T.buf[:, 0:8], T.buf[:, 8:16], A.add))
-    vsync()
-    dv(v.tensor_tensor(T.tot[:], T.t8[:, 0:4], T.t8[:, 4:8], A.add))
-    vsync()
-    for h in range(2):
-        dv(v.tensor_scalar(T.nv[:, h:h + 1], T.tot[:, h:h + 1], T.tot[:, h:h + 1], T.tot[:, 2 + h:3 + h], A.mult, A.add))
-    vsync()
-    for h in range(2):
-        o = h * (K + 1)
-        dv(v.tensor_scalar(T.fb[:, o:o + K], T.tneg[:], T.nv[:, h:h + 1], 0.5, A.is_lt, A.max))
-    vsync()
-    for h in range(2):
-        o = h * (K + 1)
-        dv(v.tensor_reduce(T.d0[:, h * L + DEG + 1:h * L + DEG + 2], T.fb[:, o:o + K + 1], AxisListType.X, A.mult))
-    vsync()
-    for h in range(2):
-        y0 = T.d0[:, h * L + DEG + 1:h * L + DEG + 2]
-        dv(v.tensor_scalar(T.gg[:, h:h + 1], T.nv[:, h:h + 1], y0, y0, A.mult, A.mult))
-    vsync()
-    for h in range(2):
-        dv(v.tensor_scalar(T.d0[:, h * L + 1:h * L + 1 + DEG], T.ones[:, 0:DEG], T.gg[:, h:h + 1], CEN, A.mult, A.add))
-    vsync()
-    dv(v.tensor_tensor_scan(T.rs[:], T.d0[:], T.d1[:], 0.0, A.mult, A.add))
-    vsync()
     v.wait_ge(S.xt, 2)
-    for h, ap in ((0, S.ap0), (1, S.ap1)):
+    v.wait_ge(S.arr, ne * len(others))
+    for h, a, b, r, sem, ap in half:
+        step(h, sem, lambda: [v.tensor_reduce(T.tot[:, j:j + 1], T.buf[:, j::4], AxisListType.X, A.add)
+                              for j in (h, 2 + h)])
+    for h, a, b, r, sem, ap in half:
+        step(h, sem, lambda: [v.tensor_scalar(a[:, K:K + 1], T.tot[:, h:h + 1], T.tot[:, h:h + 1],
+                                              T.tot[:, 2 + h:3 + h], A.mult, A.add)])
+    for h, a, b, r, sem, ap in half:
+        step(h, sem, lambda: [v.tensor_scalar(a[:, 0:K], T.tneg[:], a[:, K:K + 1], 0.25, A.is_lt, A.max),
+                              v.tensor_scalar(b[:, LA:LA + K], T.tneg[:], a[:, K:K + 1], 0.5, A.is_lt, A.max)])
+    for h, a, b, r, sem, ap in half:
+        step(h, sem, lambda: [v.tensor_tensor_scan(b[:, 0:LA], a[:], T.da[:], S2, A.mult, A.add)])
+    for h, a, b, r, sem, ap in half:
+        step(h, sem, lambda: [v.tensor_tensor_scan(r[:], b[:, K + 1:LA + K], T.db[:], 0.0, A.mult, A.add)])
+    for h, a, b, r, sem, ap in half:
+        v.wait_ge(sem, hc[h])
         v.tensor_scalar(T.yt[:, 128 * h:128 * h + 128], T.ps_xt[:, 128 * h:128 * h + 128], T.tot[:, h:h + 1],
-                        T.rs[:, h * L + L - 1:h * L + L], A.subtract, A.mult).then_inc(ap, 1)
+                        r[:, LB - 1:LB], A.subtract, A.mult).then_inc(ap, 1)
 
     pe.wait_ge(S.ap0, 1)
     pe.transpose(T.ps_y0[:, 0:128], T.yt[:, 0:128], T.ident[:]).then_inc(S.ty0, 1)

import numpy as np
from concourse.bass import DstId, RemoteDMATransfer
from concourse.mybir import AluOpType, AxisListType, ActivationFunctionType

EPS = 0.01
K = 31
DEG = 11
TAU = 0.036
S2 = 64.0
CEN = S2 * TAU * 5.0 / 8.0
HW = S2 * TAU * 3.0 / 8.0
LA = K + 2 + DEG
LB = DEG + 1 + K


def _coefs():
    ch = np.polynomial.chebyshev.Chebyshev.interpolate(lambda z: (CEN - z) ** -0.5 * np.sqrt(S2), DEG,
                                                       domain=[-1.04 * HW, 1.04 * HW])
    return [float(c) for c in ch.convert(kind=np.polynomial.Polynomial, domain=[-1, 1], window=[-1, 1]).coef]


SCRATCH = {
    "xs": ("sbuf", [128, 256], "float32"),
    "sq": ("sbuf", [128, 256], "float32"),
    "cvec": ("sbuf", [128, 2], "float32"),
    "epsadd": ("sbuf", [128, 4], "float32"),
    "buf": ("sbuf", [128, 16], "float32"),
    "ones": ("sbuf", [128, 128], "float32"),
    "ident": ("sbuf", [128, 128], "float32"),
    "tot": ("sbuf", [128, 4], "float32"),
    "four": ("sbuf", [128, K], "float32"),
    "tneg": ("sbuf", [128, K], "float32"),
    "a0": ("sbuf", [128, LA], "float32"),
    "a1": ("sbuf", [128, LA], "float32"),
    "da": ("sbuf", [128, LA], "float32"),
    "b0": ("sbuf", [128, LA + K], "float32"),
    "b1": ("sbuf", [128, LA + K], "float32"),
    "db": ("sbuf", [128, LB], "float32"),
    "r0": ("sbuf", [128, LB], "float32"),
    "r1": ("sbuf", [128, LB], "float32"),
    "yt": ("sbuf", [128, 256], "float32"),
    "ys": ("sbuf", [128, 256], "float32"),
    "ps_stat": ("psum", [128, 512], "float32"),
    "ps_xt": ("psum", [128, 512], "float32"),
    "ps_y0": ("psum", [128, 512], "float32"),
    "ps_y1": ("psum", [128, 512], "float32"),
}
SEMAPHORES = ["ld", "crhs", "cones", "idn", "sq0", "sq1", "mm", "slot", "dvc", "h0", "h1", "arr", "sent", "xt",
              "ap0", "ap1", "ty0", "ty1", "cp0", "cp1", "st"]


def rank_program(g, core, T, topo):
    rank = T.rank_of(core)
    if rank is None:
        return
    S = T.sem
    v, pe, act, sy = g.vector, g.tensor, g.scalar, g.sync
    n = len(T.cores)
    d = 128 * n
    A = AluOpType
    co = _coefs()

    def place(c):
        return (topo.host(c), topo.chip(c))

    others = [c for c in T.cores if c != core and place(c) != place(core)]
    others += [c for c in T.cores if c != core and place(c) == place(core)]

    sy.dma_start(T.xs[:], T.x[:]).then_inc(S.ld, 16)

    cc = [0]

    def cst(ins):
        ins.then_inc(S.dvc, 1)
        cc[0] += 1

    v.memset(T.cvec[:, 0:1], 1.0 / d).then_inc(S.crhs, 1)
    v.memset(T.cvec[:, 1:2], -1.0 / d).then_inc(S.crhs, 1)
    v.memset(T.ones[:], 1.0).then_inc(S.cones, 1)
    g.wait_ge(S.cones, 1)
    g.affine_select(T.ident[:], T.ones[:], [[-1, 128]], A.is_equal, 0.0, 0, 1).then_inc(S.idn, 1)
    cst(v.memset(T.four[:], 4.0))
    cst(v.memset(T.da[:, 0:K + 1], 0.0))
    cst(v.memset(T.epsadd[:, 0:2], 0.0))
    cst(v.memset(T.epsadd[:, 2:4], -EPS / n))
    cst(v.memset(T.da[:, K + 1:K + 2], CEN))
    cst(v.memset(T.da[:, K + 2:LA], 0.0))
    cst(v.memset(T.a0[:, K + 1:LA], 1.0))
    cst(v.memset(T.a1[:, K + 1:LA], 1.0))
    cst(v.memset(T.db[:, DEG + 1:LB], 0.0))
    for j in range(DEG + 1):
        cst(v.memset(T.db[:, j:j + 1], co[DEG - j]))
    v.wait_ge(S.dvc, cc[0])
    cst(v.tensor_tensor_scan(T.tneg[:], T.four[:], T.da[:, 0:K], -TAU / 4.0, A.mult, A.add))

    act.wait_ge(S.ld, 16)
    for h, s in ((0, S.sq0), (1, S.sq1)):
        act.activation(T.sq[:, 128 * h:128 * h + 128], T.xs[:, 128 * h:128 * h + 128],
                       ActivationFunctionType.Square).then_inc(s, 1)
    pe.wait_ge(S.ld, 16)
    pe.wait_ge(S.crhs, 2)
    for h in range(2):
        pe.matmul(T.ps_stat[:, h:h + 1], T.xs[:, 128 * h:128 * h + 128], T.cvec[:, 0:1], True, True).then_inc(S.mm, 1)
    for h, s in ((0, S.sq0), (1, S.sq1)):
        pe.wait_ge(s, 1)
        pe.matmul(T.ps_stat[:, 2 + h:3 + h], T.sq[:, 128 * h:128 * h + 128], T.cvec[:, 1:2], True, True).then_inc(S.mm, 1)
    v.wait_ge(S.mm, 4)
    mine = T.buf[:, 4 * rank:4 * rank + 4]
    v.tensor_tensor(mine, T.ps_stat[:, 0:4], T.epsadd[:], A.add).then_inc(S.slot, 1)

    mask = -1
    for c in others:
        mask &= topo.mask(core, c)
    ne = bin(mask).count("1")
    ids = []
    for c in others:
        rid, pid = topo.addr(c, core)
        ids.append(DstId(rid=rid, pnc=pid))
    g.wait_ge(S.slot, 1)
    g.remote_dma_fused([RemoteDMATransfer(dst_ids=ids, dma_engine_mask=mask, remote_sem=S.arr, srcs=[mine],
                                          dsts=[mine for _ in others], alu_op=0)], local_sem=S.sent)

    pe.wait_ge(S.idn, 1)
    for h in range(2):
        pe.transpose(T.ps_xt[:, 128 * h:128 * h + 128], T.xs[:, 128 * h:128 * h + 128], T.ident[:]).then_inc(S.xt, 1)

    half = ((0, T.a0, T.b0, T.r0, S.h0, S.ap0), (1, T.a1, T.b1, T.r1, S.h1, S.ap1))
    hc = [0, 0]

    def step(h, sem, calls):
        if hc[h]:
            v.wait_ge(sem, hc[h])
        for ins in calls():
            ins.then_inc(sem, 1)
            hc[h] += 1

    v.wait_ge(S.dvc, cc[0])
    v.wait_ge(S.slot, 1)
    v.wait_ge(S.xt, 2)
    v.wait_ge(S.arr, ne * len(others))
    for h, a, b, r, sem, ap in half:
        step(h, sem, lambda: [v.tensor_reduce(T.tot[:, j:j + 1], T.buf[:, j::4], AxisListType.X, A.add)
                              for j in (h, 2 + h)])
    for h, a, b, r, sem, ap in half:
        step(h, sem, lambda: [v.tensor_scalar(a[:, K:K + 1], T.tot[:, h:h + 1], T.tot[:, h:h + 1],
                                              T.tot[:, 2 + h:3 + h], A.mult, A.add)])
    for h, a, b, r, sem, ap in half:
        step(h, sem, lambda: [v.tensor_scalar(a[:, 0:K], T.tneg[:], a[:, K:K + 1], 0.25, A.is_lt, A.max),
                              v.tensor_scalar(b[:, LA:LA + K], T.tneg[:], a[:, K:K + 1], 0.5, A.is_lt, A.max)])
    for h, a, b, r, sem, ap in half:
        step(h, sem, lambda: [v.tensor_tensor_scan(b[:, 0:LA], a[:], T.da[:], S2, A.mult, A.add)])
    for h, a, b, r, sem, ap in half:
        step(h, sem, lambda: [v.tensor_tensor_scan(r[:], b[:, K + 1:LA + K], T.db[:], 0.0, A.mult, A.add)])
    for h, a, b, r, sem, ap in half:
        v.wait_ge(sem, hc[h])
        v.tensor_scalar(T.yt[:, 128 * h:128 * h + 128], T.ps_xt[:, 128 * h:128 * h + 128], T.tot[:, h:h + 1],
                        r[:, LB - 1:LB], A.subtract, A.mult).then_inc(ap, 1)

    pe.wait_ge(S.ap0, 1)
    pe.transpose(T.ps_y0[:, 0:128], T.yt[:, 0:128], T.ident[:]).then_inc(S.ty0, 1)
    pe.wait_ge(S.ap1, 1)
    pe.transpose(T.ps_y1[:, 0:128], T.yt[:, 128:256], T.ident[:]).then_inc(S.ty1, 1)
    v.wait_ge(S.ty0, 1)
    v.tensor_copy(T.ys[:, 0:128], T.ps_y0[:, 0:128]).then_inc(S.cp0, 1)
    v.wait_ge(S.ty1, 1)
    v.tensor_copy(T.ys[:, 128:256], T.ps_y1[:, 0:128]).then_inc(S.cp1, 1)
    sy.wait_ge(S.cp0, 1)
    sy.dma_start(T.y[:, 0:128], T.ys[:, 0:128]).then_inc(S.st, 16)
    act.wait_ge(S.cp1, 1)
    act.dma_start(T.y[:, 128:256], T.ys[:, 128:256]).then_inc(S.st, 16)
    g.wait_ge(S.sent, ne)
    sy.wait_ge(S.st, 32)
